import numpy as np
import ml_dtypes


def mxq(x, axis, fmt="e4m3"):
    dtype, down = {"e4m3": (ml_dtypes.float8_e4m3fn, 7), "e5m2": (ml_dtypes.float8_e5m2, 14)}[fmt]
    v = np.moveaxis(np.asarray(x, np.float32).astype(ml_dtypes.bfloat16).astype(np.float64), axis, -1)
    blocks = v.reshape(v.shape[:-1] + (-1, 32))
    amax = np.abs(blocks).max(-1, keepdims=True)
    byte = np.maximum(np.where(amax > 0, np.frexp(amax)[1] - 1 + 127, 0) - down, 1)
    scale = np.exp2(byte - 127.0)
    codes = (blocks / scale).astype(np.float32).astype(dtype).astype(np.float64)
    return np.moveaxis((codes * scale).reshape(v.shape), -1, axis)


WIDE = False


def mx_kscale(k):
    if not WIDE:
        return np.ones(k)
    levels = np.array([30, -30])
    if k % 512:
        return np.exp2(np.random.permutation(np.resize(levels, k // 32))).repeat(32)
    a = np.empty((k // 512, 16))
    for p in range(k // 512):
        a[p, :8] = np.random.permutation(np.resize(levels, 8))
        for g in range(8):
            far = levels[np.abs(levels - a[p, g]) >= 10]
            a[p, g + 8] = far[np.random.randint(len(far))]
    return np.exp2(a.ravel()).repeat(32)


def f64(x):
    return np.asarray(x).astype(np.float64)


E2M1 = np.array([0.0, 0.5, 1.0, 1.5, 2.0, 3.0, 4.0, 6.0, -0.0, -0.5, -1.0, -1.5, -2.0, -3.0, -4.0, -6.0])


def pack_weight(w, fmt):
    k, n = w.shape
    w = f64(np.asarray(w, np.float32).astype(ml_dtypes.bfloat16)).reshape(k // 32, 32, n)
    amax = np.abs(w).max(1)
    if fmt == "e4m3":
        byte = np.frexp(amax)[1] - 1 + 127 - 7
    else:
        mant, ex = np.frexp(amax / 6.0)
        byte = np.where(mant > 0.5, ex, ex - 1) + 127
    byte = np.clip(np.where(amax > 0, byte, 1), 1, 254)
    scaled = (w * np.exp2(127.0 - byte)[:, None, :]).reshape(k, n).astype(np.float32)
    by_word = np.ascontiguousarray(scaled.reshape(k // 512, 128, 4, n).transpose(0, 1, 3, 2))
    if fmt == "e4m3":
        words = by_word.astype(ml_dtypes.float8_e4m3fn).view(np.uint8)
    else:
        c = by_word.astype(ml_dtypes.float4_e2m1fn).view(np.uint8) & 0xF
        words = (c[..., 0::2] | (c[..., 1::2] << 4)).reshape(k // 512, 128, 2 * n)
    return np.ascontiguousarray(words), np.ascontiguousarray(byte.astype(np.uint8).reshape(k // 512, 16, n))


def unpack_weight(words, scales, fmt):
    g, _, n = scales.shape
    words = np.ascontiguousarray(words).reshape(g, 128, n, -1)
    if fmt == "e4m3":
        vals = words.view(ml_dtypes.float8_e4m3fn).astype(np.float64)
    else:
        nib = np.empty((g, 128, n, 4), np.uint8)
        nib[..., 0::2] = words & 0xF
        nib[..., 1::2] = words >> 4
        vals = E2M1[nib]
    vals = vals * np.repeat(np.exp2(scales.astype(np.float64) - 127.0), 8, axis=1)[..., None]
    return vals.transpose(0, 1, 3, 2).reshape(g * 512, n)


N, R, K, T = 1024, 512, 1024, 512


def setup_inputs():
    n = np.random.standard_normal
    s = mx_kscale(N)[:, None]
    u = mx_kscale(R)[:, None]
    m = np.exp(0.5 * n((1, T)))
    w = n((N, K)) / np.sqrt(N) / s
    p_w8 = pack_weight(w[:512], "e4m3")
    p_w4 = pack_weight(w[512:], "e2m1")
    return {
        "dy": (m * n((N, T)) * s).astype(np.float32),
        "w8_words": p_w8[0],
        "w8_scales": p_w8[1],
        "w4_words": p_w4[0],
        "w4_scales": p_w4[1],
        "bu": (n((N, R)) / np.sqrt(N) / s * u.T).astype(np.float32),
        "ad": (0.5 * n((R, K)) / np.sqrt(R) / u).astype(np.float32),
        "d": (0.5 + 0.3 * n((K, T))).astype(np.float32),
    }


def reference(dy, w8_words, w8_scales, w4_words, w4_scales, bu, ad, d):
    dy_ = mxq(f64(dy), 0, "e5m2")
    w8_ = unpack_weight(w8_words, w8_scales, "e4m3")
    w4_ = unpack_weight(w4_words, w4_scales, "e2m1")
    bu_ = mxq(f64(bu), 0, "e4m3")
    h = bu_.T @ dy_
    h_ = mxq(h, 0, "e5m2")
    ad_ = mxq(f64(ad), 0, "e4m3")
    dx = w8_.T @ dy_[:512] + w4_.T @ dy_[512:] + ad_.T @ h_
    return dx * f64(d), h

@@ -1,0 +1,210 @@
+from contextlib import ExitStack
+
+import concourse.mybir as mybir
+
+N, R, K, T = 1024, 512, 1024, 512
+FLOPS = 2 * (N * R * T + N * K * T + R * K * T)
+
+F32 = mybir.dt.float32
+BF16 = mybir.dt.bfloat16
+I32 = mybir.dt.int32
+U32 = mybir.dt.uint32
+U8 = mybir.dt.uint8
+E4M3 = mybir.dt.float8_e4m3fn_x4
+E5M2 = mybir.dt.float8_e5m2_x4
+E2M1 = mybir.dt.float4_e2m1fn_x4
+
+P = 128
+PACK = 4
+PASS = P * PACK
+HALF = K // 2
+TILES = K // P
+VECTOR_COLS = 352
+VECTOR_AD_COLS = 256
+VECTOR_SLOTS = 3
+
+
+def interleave(copy, grouped, raw, c0, c1):
+    copy(
+        out=grouped[:, c0:c1, :].rearrange("p (c i) j -> p c j i", i=4),
+        in_=raw[:, :, c0:c1].rearrange("p j (c i) -> p c j i", i=4),
+    )
+
+
+def interleave_by_slot(copy, grouped, raw, s0, s1):
+    copy(
+        out=grouped[:, s0:s1, :, :].rearrange("p s m j -> p m j s"),
+        in_=raw[:].rearrange("p j (m s) -> p m j s", s=PACK)[:, :, :, s0:s1],
+    )
+
+
+def tile_mix_lrbwd_mix_mul_kernel(
+    tc, dy, w8_words, w8_scales, w4_words, w4_scales, bu, ad, d, out_0, out_1
+):
+    nc = tc.nc
+    with ExitStack() as ctx:
+        sb = ctx.enter_context(tc.tile_pool(name="sb", bufs=1))
+        ps = ctx.enter_context(tc.psum_pool(name="ps", bufs=1))
+        ctx.enter_context(tc.manual_schedule())
+
+        def tile(name, shape, dtype):
+            return sb.tile(shape, dtype, name=name, tag=name, align_bytes=64)
+
+        def quantize(codes, scales, grouped, fmt):
+            nc.vector.quantize_mx(out=codes.bitcast(fmt), scales=scales, in_=grouped)
+
+        dy_raw = [tile("dy_raw%d" % g, [P, PACK, T], F32) for g in range(2)]
+        bu_raw = [tile("bu_raw%d" % g, [P, PACK, R], F32) for g in range(2)]
+        ad_raw = [tile("ad_raw%d" % u, [P, PACK, HALF], F32) for u in range(2)]
+        d_sb = [tile("d_sb%d" % u, [P, TILES // 2, T], F32) for u in range(2)]
+        w8_codes = tile("w8_codes", [P, K], U32)
+        w4_codes = tile("w4_codes", [P, 2 * K], U8)
+        w_planes = tile("w_planes", [P, 2 * K], U8)
+        w8_plane = w_planes[:, 0:K]
+        w4_plane = w_planes[:, K : 2 * K]
+
+        nc.vector.memset(w_planes[:].bitcast(U32), 0)
+
+        def load_rows(dst, rows):
+            nc.sync.dma_start(out=dst[:], in_=rows.rearrange("(p j) c -> p j c", j=PACK))
+
+        def load_scale_rows(plane, scales, q):
+            nc.sync.dma_start(
+                out=plane[32 * q : 32 * q + 4, :].bitcast(I32),
+                in_=scales[0, 4 * q : 4 * q + 4, :].bitcast(I32),
+            )
+
+        load_rows(dy_raw[0], dy[0:PASS, :])
+        load_rows(bu_raw[0], bu[0:PASS, :])
+        load_scale_rows(w8_plane, w8_scales, 0)
+        load_rows(dy_raw[1], dy[PASS:N, :])
+        load_scale_rows(w8_plane, w8_scales, 1)
+        load_rows(bu_raw[1], bu[PASS:N, :])
+        load_scale_rows(w8_plane, w8_scales, 2)
+        load_scale_rows(w8_plane, w8_scales, 3)
+        nc.sync.dma_start(
+            out=w8_codes[:].bitcast(I32),
+            in_=w8_words[0].rearrange("p k i -> p (k i)").bitcast(I32),
+        )
+        load_scale_rows(w4_plane, w4_scales, 0)
+        load_scale_rows(w4_plane, w4_scales, 1)
+        nc.sync.dma_start(out=w4_codes[:].bitcast(I32), in_=w4_words[0].bitcast(I32))
+        load_scale_rows(w4_plane, w4_scales, 2)
+        load_scale_rows(w4_plane, w4_scales, 3)
+        for u in range(2):
+            load_rows(ad_raw[u], ad[:, u * HALF : (u + 1) * HALF])
+        for u in range(2):
+            nc.sync.dma_start(
+                out=d_sb[u][:],
+                in_=d[u * HALF : (u + 1) * HALF, :].rearrange("(m p) t -> p m t", p=P),
+            )
+
+        dy_codes = [tile("dy_codes%d" % g, [P, T], U32) for g in range(2)]
+        dy_plane = [tile("dy_plane%d" % g, [P, T], U8) for g in range(2)]
+        bu_codes = [tile("bu_codes%d" % g, [P, R], U32) for g in range(2)]
+        bu_plane = [tile("bu_plane%d" % g, [P, R], U8) for g in range(2)]
+        h_acc = [ps.tile([P, T], F32, name="h_acc%d" % s, tag="bank%d" % (4 + s)) for s in range(PACK)]
+
+        for g in range(2):
+            dy_bf = tile("dy_bf%d" % g, [P, T, PACK], BF16)
+            interleave(nc.vector.tensor_copy, dy_bf, dy_raw[g], 0, VECTOR_COLS)
+            interleave(nc.scalar.copy, dy_bf, dy_raw[g], VECTOR_COLS, T)
+            quantize(dy_codes[g][:], dy_plane[g][:], dy_bf[:].rearrange("p c j -> p (c j)"), E5M2)
+
+            bu_bf = tile("bu_bf%d" % g, [P, PACK, P, PACK], BF16)
+            interleave_by_slot(nc.vector.tensor_copy, bu_bf, bu_raw[g], 0, VECTOR_SLOTS)
+            interleave_by_slot(nc.scalar.copy, bu_bf, bu_raw[g], VECTOR_SLOTS, PACK)
+            for s0 in (0, 2):
+                cols = slice(s0 * P, (s0 + 2) * P)
+                quantize(
+                    bu_codes[g][:, cols],
+                    bu_plane[g][:, cols],
+                    bu_bf[:, s0 : s0 + 2, :, :].rearrange("p s m j -> p (s m j)"),
+                    E4M3,
+                )
+            for s in range(PACK):
+                cols = slice(s * P, (s + 1) * P)
+                nc.tensor.matmul_mx(
+                    out=h_acc[s][:],
+                    lhsT=bu_codes[g][:, cols].bitcast(E4M3),
+                    lhsT_scale=bu_plane[g][:, cols],
+                    rhs=dy_codes[g][:].bitcast(E5M2),
+                    rhs_scale=dy_plane[g][:],
+                    start=(g == 0),
+                    stop=(g == 1),
+                )
+
+        h_sb = tile("h_sb", [P, PACK, T], F32)
+        for s in range(PACK):
+            copy = nc.scalar.copy if s % 2 == 0 else nc.vector.tensor_copy
+            copy(out=h_sb[:, s, :], in_=h_acc[s][:])
+
+        dx_acc = []
+        for m in range(TILES):
+            acc = ps.tile([P, T], F32, name="dx_acc%d" % m, tag="bank%d" % m)
+            dx_acc.append(acc)
+            cols = slice(m * P, (m + 1) * P)
+            nc.tensor.matmul_mx(
+                out=acc[:],
+                lhsT=w8_codes[:, cols].bitcast(E4M3),
+                lhsT_scale=w8_plane[:, cols],
+                rhs=dy_codes[0][:].bitcast(E5M2),
+                rhs_scale=dy_plane[0][:],
+                start=True,
+                stop=False,
+            )
+            nc.tensor.matmul_mx(
+                out=acc[:],
+                lhsT=w4_codes[:, 2 * m * P : 2 * (m + 1) * P].bitcast(E2M1),
+                lhsT_scale=w4_plane[:, cols],
+                rhs=dy_codes[1][:].bitcast(E5M2),
+                rhs_scale=dy_plane[1][:],
+                start=False,
+                stop=False,
+            )
+
+        h_bf = tile("h_bf", [P, T, PACK], BF16)
+        h_codes = tile("h_codes", [P, T], U32)
+        h_plane = tile("h_plane", [P, T], U8)
+        ad_bf = [tile("ad_bf%d" % u, [P, HALF, PACK], BF16) for u in range(2)]
+        ad_codes = [tile("ad_codes%d" % u, [P, HALF], U32) for u in range(2)]
+        ad_plane = [tile("ad_plane%d" % u, [P, HALF], U8) for u in range(2)]
+
+        def cast_ad(u):
+            interleave(nc.vector.tensor_copy, ad_bf[u], ad_raw[u], 0, VECTOR_AD_COLS)
+            interleave(nc.scalar.copy, ad_bf[u], ad_raw[u], VECTOR_AD_COLS, HALF)
+
+        def quantize_ad(u):
+            quantize(ad_codes[u][:], ad_plane[u][:], ad_bf[u][:].rearrange("p c j -> p (c j)"), E4M3)
+
+        interleave(nc.vector.tensor_copy, h_bf, h_sb, 0, VECTOR_COLS)
+        interleave(nc.scalar.copy, h_bf, h_sb, VECTOR_COLS, T)
+        cast_ad(0)
+        quantize(h_codes[:], h_plane[:], h_bf[:].rearrange("p c j -> p (c j)"), E5M2)
+        quantize_ad(0)
+        cast_ad(1)
+        quantize_ad(1)
+
+        nc.sync.dma_start(out=out_1.rearrange("(p s) t -> p s t", s=PACK), in_=h_sb[:])
+
+        for u in range(2):
+            res = tile("res%d" % u, [P, TILES // 2, T], F32)
+            for i in range(TILES // 2):
+                acc = dx_acc[u * (TILES // 2) + i]
+                cols = slice(i * P, (i + 1) * P)
+                nc.tensor.matmul_mx(
+                    out=acc[:],
+                    lhsT=ad_codes[u][:, cols].bitcast(E4M3),
+                    lhsT_scale=ad_plane[u][:, cols],
+                    rhs=h_codes[:].bitcast(E5M2),
+                    rhs_scale=h_plane[:],
+                    start=False,
+                    stop=True,
+                )
+                nc.vector.tensor_tensor(
+                    out=res[:, i, :], in0=acc[:], in1=d_sb[u][:, i, :], op=mybir.AluOpType.mult
+                )
+            nc.sync.dma_start(
+                out=out_0[u * HALF : (u + 1) * HALF, :].rearrange("(m p) t -> p m t", p=P),
+                in_=res[:],
+            )

@@ -20,8 +20,6 @@ PASS = P * PACK
 HALF = K // 2
 TILES = K // P
 VECTOR_COLS = 352
-VECTOR_AD_COLS = 256
-VECTOR_SLOTS = 3
 
 
 def interleave(copy, grouped, raw, c0, c1):
@@ -34,7 +32,7 @@ def interleave(copy, grouped, raw, c0, c1):
 def interleave_by_slot(copy, grouped, raw, s0, s1):
     copy(
         out=grouped[:, s0:s1, :, :].rearrange("p s m j -> p m j s"),
-        in_=raw[:].rearrange("p j (m s) -> p m j s", s=PACK)[:, :, :, s0:s1],
+        in_=raw.rearrange("p j (m s) -> p m j s", s=PACK)[:, :, :, s0:s1],
     )
 
 
@@ -55,15 +53,19 @@ def tile_mix_lrbwd_mix_mul_kernel(
 
         dy_raw = [tile("dy_raw%d" % g, [P, PACK, T], F32) for g in range(2)]
         bu_raw = [tile("bu_raw%d" % g, [P, PACK, R], F32) for g in range(2)]
-        ad_raw = [tile("ad_raw%d" % u, [P, PACK, HALF], F32) for u in range(2)]
+        ad_raw = tile("ad_raw", [P, PACK, K], F32)
         d_sb = [tile("d_sb%d" % u, [P, TILES // 2, T], F32) for u in range(2)]
+        w8_raw = tile("w8_raw", [P, K], U32)
+        w4_raw = tile("w4_raw", [P, 2 * K], U8)
+        planes_raw = tile("planes_raw", [P, 2 * K], U8)
+        w8_plane_raw = planes_raw[:, 0:K]
+        w4_plane_raw = planes_raw[:, K : 2 * K]
         w8_codes = tile("w8_codes", [P, K], U32)
         w4_codes = tile("w4_codes", [P, 2 * K], U8)
-        w_planes = tile("w_planes", [P, 2 * K], U8)
-        w8_plane = w_planes[:, 0:K]
-        w4_plane = w_planes[:, K : 2 * K]
+        w8_plane = tile("w8_plane", [P, K], U8)
+        w4_plane = tile("w4_plane", [P, K], U8)
 
-        nc.vector.memset(w_planes[:].bitcast(U32), 0)
+        nc.vector.memset(planes_raw[:].bitcast(U32), 0)
 
         def load_rows(dst, rows):
             nc.sync.dma_start(out=dst[:], in_=rows.rearrange("(p j) c -> p j c", j=PACK))
@@ -75,28 +77,26 @@ def tile_mix_lrbwd_mix_mul_kernel(
             )
 
         load_rows(dy_raw[0], dy[0:PASS, :])
+        for q in range(4):
+            load_scale_rows(w8_plane_raw, w8_scales, q)
         load_rows(bu_raw[0], bu[0:PASS, :])
-        load_scale_rows(w8_plane, w8_scales, 0)
+        for q in range(4):
+            load_scale_rows(w4_plane_raw, w4_scales, q)
         load_rows(dy_raw[1], dy[PASS:N, :])
-        load_scale_rows(w8_plane, w8_scales, 1)
         load_rows(bu_raw[1], bu[PASS:N, :])
-        load_scale_rows(w8_plane, w8_scales, 2)
-        load_scale_rows(w8_plane, w8_scales, 3)
         nc.sync.dma_start(
-            out=w8_codes[:].bitcast(I32),
+            out=w8_raw[:].bitcast(I32),
             in_=w8_words[0].rearrange("p k i -> p (k i)").bitcast(I32),
         )
-        load_scale_rows(w4_plane, w4_scales, 0)
-        load_scale_rows(w4_plane, w4_scales, 1)
-        nc.sync.dma_start(out=w4_codes[:].bitcast(I32), in_=w4_words[0].bitcast(I32))
-        load_scale_rows(w4_plane, w4_scales, 2)
-        load_scale_rows(w4_plane, w4_scales, 3)
+        nc.sync.dma_start(out=w4_raw[:].bitcast(I32), in_=w4_words[0].bitcast(I32))
+        load_rows(ad_raw, ad)
         for u in range(2):
-            load_rows(ad_raw[u], ad[:, u * HALF : (u + 1) * HALF])
-        for u in range(2):
-            nc.sync.dma_start(
-                out=d_sb[u][:],
-                in_=d[u * HALF : (u + 1) * HALF, :].rearrange("(m p) t -> p m t", p=P),
+            load_rows(d_sb[u], d[u * HALF : (u + 1) * HALF, :])
+
+        def sort_plane(plane, raw):
+            nc.vector.tensor_copy(
+                out=plane[:].rearrange("p (u s m) -> p u s m", u=2, s=PACK),
+                in_=raw.rearrange("p (u m s) -> p u s m", u=2, s=PACK),
             )
 
         dy_codes = [tile("dy_codes%d" % g, [P, T], U32) for g in range(2)]
@@ -109,11 +109,15 @@ def tile_mix_lrbwd_mix_mul_kernel(
             dy_bf = tile("dy_bf%d" % g, [P, T, PACK], BF16)
             interleave(nc.vector.tensor_copy, dy_bf, dy_raw[g], 0, VECTOR_COLS)
             interleave(nc.scalar.copy, dy_bf, dy_raw[g], VECTOR_COLS, T)
+            if g == 0:
+                sort_plane(w8_plane, w8_plane_raw)
             quantize(dy_codes[g][:], dy_plane[g][:], dy_bf[:].rearrange("p c j -> p (c j)"), E5M2)
 
             bu_bf = tile("bu_bf%d" % g, [P, PACK, P, PACK], BF16)
-            interleave_by_slot(nc.vector.tensor_copy, bu_bf, bu_raw[g], 0, VECTOR_SLOTS)
-            interleave_by_slot(nc.scalar.copy, bu_bf, bu_raw[g], VECTOR_SLOTS, PACK)
+            interleave_by_slot(nc.vector.tensor_copy, bu_bf, bu_raw[g][:], 0, 2)
+            interleave_by_slot(nc.scalar.copy, bu_bf, bu_raw[g][:], 2, PACK)
+            if g == 0:
+                sort_plane(w4_plane, w4_plane_raw)
             for s0 in (0, 2):
                 cols = slice(s0 * P, (s0 + 2) * P)
                 quantize(
@@ -134,9 +138,18 @@ def tile_mix_lrbwd_mix_mul_kernel(
                     stop=(g == 1),
                 )
 
+        nc.vector.tensor_copy(
+            out=w8_codes[:].bitcast(I32).rearrange("p (u s m) -> p u m s", u=2, s=PACK),
+            in_=w8_raw[:].bitcast(I32).rearrange("p (u m s) -> p u m s", u=2, s=PACK),
+        )
+        nc.vector.tensor_copy(
+            out=w4_codes[:].rearrange("p (u s m b) -> p u s m b", u=2, s=PACK, b=2),
+            in_=w4_raw[:].rearrange("p (u m s b) -> p u s m b", u=2, s=PACK, b=2),
+        )
+
         h_sb = tile("h_sb", [P, PACK, T], F32)
         for s in range(PACK):
-            copy = nc.scalar.copy if s % 2 == 0 else nc.vector.tensor_copy
+            copy = nc.scalar.copy if s < PACK - 1 else nc.vector.tensor_copy
             copy(out=h_sb[:, s, :], in_=h_acc[s][:])
 
         dx_acc = []
@@ -166,45 +179,61 @@ def tile_mix_lrbwd_mix_mul_kernel(
         h_bf = tile("h_bf", [P, T, PACK], BF16)
         h_codes = tile("h_codes", [P, T], U32)
         h_plane = tile("h_plane", [P, T], U8)
-        ad_bf = [tile("ad_bf%d" % u, [P, HALF, PACK], BF16) for u in range(2)]
+        ad_bf = [tile("ad_bf%d" % u, [P, PACK, P, PACK], BF16) for u in range(2)]
         ad_codes = [tile("ad_codes%d" % u, [P, HALF], U32) for u in range(2)]
         ad_plane = [tile("ad_plane%d" % u, [P, HALF], U8) for u in range(2)]
 
         def cast_ad(u):
-            interleave(nc.vector.tensor_copy, ad_bf[u], ad_raw[u], 0, VECTOR_AD_COLS)
-            interleave(nc.scalar.copy, ad_bf[u], ad_raw[u], VECTOR_AD_COLS, HALF)
+            raw = ad_raw[:, :, u * HALF : (u + 1) * HALF]
+            interleave_by_slot(nc.vector.tensor_copy, ad_bf[u], raw, 0, 2)
+            interleave_by_slot(nc.scalar.copy, ad_bf[u], raw, 2, PACK)
 
-        def quantize_ad(u):
-            quantize(ad_codes[u][:], ad_plane[u][:], ad_bf[u][:].rearrange("p c j -> p (c j)"), E4M3)
+        def quantize_ad(u, s0, s1):
+            cols = slice(s0 * P, s1 * P)
+            quantize(
+                ad_codes[u][:, cols],
+                ad_plane[u][:, cols],
+                ad_bf[u][:, s0:s1, :, :].rearrange("p s m j -> p (s m j)"),
+                E4M3,
+            )
+
+        res = [tile("res%d" % u, [P, PACK, T], F32) for u in range(2)]
+
+        def finish(u, s):
+            acc = dx_acc[u * PACK + s]
+            cols = slice(s * P, (s + 1) * P)
+            nc.tensor.matmul_mx(
+                out=acc[:],
+                lhsT=ad_codes[u][:, cols].bitcast(E4M3),
+                lhsT_scale=ad_plane[u][:, cols],
+                rhs=h_codes[:].bitcast(E5M2),
+                rhs_scale=h_plane[:],
+                start=False,
+                stop=True,
+            )
+            nc.vector.tensor_tensor(
+                out=res[u][:, s, :], in0=acc[:], in1=d_sb[u][:, s, :], op=mybir.AluOpType.mult
+            )
+
+        def store(u, s0, s1):
+            rows = out_0[u * HALF : (u + 1) * HALF, :].rearrange("(p s) t -> p s t", s=PACK)
+            nc.sync.dma_start(out=rows[:, s0:s1, :], in_=res[u][:, s0:s1, :])
 
         interleave(nc.vector.tensor_copy, h_bf, h_sb, 0, VECTOR_COLS)
         interleave(nc.scalar.copy, h_bf, h_sb, VECTOR_COLS, T)
-        cast_ad(0)
         quantize(h_codes[:], h_plane[:], h_bf[:].rearrange("p c j -> p (c j)"), E5M2)
-        quantize_ad(0)
+        cast_ad(0)
         cast_ad(1)
-        quantize_ad(1)
+        quantize_ad(0, 0, PACK)
+        quantize_ad(1, 0, 2)
 
         nc.sync.dma_start(out=out_1.rearrange("(p s) t -> p s t", s=PACK), in_=h_sb[:])
 
-        for u in range(2):
-            res = tile("res%d" % u, [P, TILES // 2, T], F32)
-            for i in range(TILES // 2):
-                acc = dx_acc[u * (TILES // 2) + i]
-                cols = slice(i * P, (i + 1) * P)
-                nc.tensor.matmul_mx(
-                    out=acc[:],
-                    lhsT=ad_codes[u][:, cols].bitcast(E4M3),
-                    lhsT_scale=ad_plane[u][:, cols],
-                    rhs=h_codes[:].bitcast(E5M2),
-                    rhs_scale=h_plane[:],
-                    start=False,
-                    stop=True,
-                )
-                nc.vector.tensor_tensor(
-                    out=res[:, i, :], in0=acc[:], in1=d_sb[u][:, i, :], op=mybir.AluOpType.mult
-                )
-            nc.sync.dma_start(
-                out=out_0[u * HALF : (u + 1) * HALF, :].rearrange("(m p) t -> p m t", p=P),
-                in_=res[:],
-            )
+        for s in range(PACK):
+            finish(0, s)
+        store(0, 0, PACK)
+        quantize_ad(1, 2, PACK)
+        for s0 in (0, 2):
+            finish(1, s0)
+            finish(1, s0 + 1)
+            store(1, s0, s0 + 2)

@@ -72,23 +72,23 @@ def tile_mix_lrbwd_mix_mul_kernel(
 
         def load_scale_rows(plane, scales, q):
             nc.sync.dma_start(
-                out=plane[32 * q : 32 * q + 4, :].bitcast(I32),
-                in_=scales[0, 4 * q : 4 * q + 4, :].bitcast(I32),
+                out=plane[q:P:32, :].bitcast(I32),
+                in_=scales[0, q:16:4, :].bitcast(I32),
             )
 
         load_rows(dy_raw[0], dy[0:PASS, :])
         for q in range(4):
             load_scale_rows(w8_plane_raw, w8_scales, q)
         load_rows(bu_raw[0], bu[0:PASS, :])
+        nc.sync.dma_start(out=w4_raw[:].bitcast(I32), in_=w4_words[0].bitcast(I32))
+        load_rows(dy_raw[1], dy[PASS:N, :])
         for q in range(4):
             load_scale_rows(w4_plane_raw, w4_scales, q)
-        load_rows(dy_raw[1], dy[PASS:N, :])
         load_rows(bu_raw[1], bu[PASS:N, :])
         nc.sync.dma_start(
             out=w8_raw[:].bitcast(I32),
             in_=w8_words[0].rearrange("p k i -> p (k i)").bitcast(I32),
         )
-        nc.sync.dma_start(out=w4_raw[:].bitcast(I32), in_=w4_words[0].bitcast(I32))
         load_rows(ad_raw, ad)
         for u in range(2):
             load_rows(d_sb[u], d[u * HALF : (u + 1) * HALF, :])
@@ -105,19 +105,46 @@ def tile_mix_lrbwd_mix_mul_kernel(
         bu_plane = [tile("bu_plane%d" % g, [P, R], U8) for g in range(2)]
         h_acc = [ps.tile([P, T], F32, name="h_acc%d" % s, tag="bank%d" % (4 + s)) for s in range(PACK)]
 
+        dx_acc = []
+
+        def w4_pass(m):
+            acc = ps.tile([P, T], F32, name="dx_acc%d" % m, tag="bank%d" % m)
+            dx_acc.append(acc)
+            nc.tensor.matmul_mx(
+                out=acc[:],
+                lhsT=w4_codes[:, 2 * m * P : 2 * (m + 1) * P].bitcast(E2M1),
+                lhsT_scale=w4_plane[:, m * P : (m + 1) * P],
+                rhs=dy_codes[1][:].bitcast(E5M2),
+                rhs_scale=dy_plane[1][:],
+                start=True,
+                stop=False,
+            )
+
+        def w8_pass(m):
+            cols = slice(m * P, (m + 1) * P)
+            nc.tensor.matmul_mx(
+                out=dx_acc[m][:],
+                lhsT=w8_codes[:, cols].bitcast(E4M3),
+                lhsT_scale=w8_plane[:, cols],
+                rhs=dy_codes[0][:].bitcast(E5M2),
+                rhs_scale=dy_plane[0][:],
+                start=False,
+                stop=False,
+            )
+
         for g in range(2):
             dy_bf = tile("dy_bf%d" % g, [P, T, PACK], BF16)
-            interleave(nc.vector.tensor_copy, dy_bf, dy_raw[g], 0, VECTOR_COLS)
-            interleave(nc.scalar.copy, dy_bf, dy_raw[g], VECTOR_COLS, T)
-            if g == 0:
-                sort_plane(w8_plane, w8_plane_raw)
+            interleave(nc.vector.tensor_copy, dy_bf, dy_raw[g], 0, T // 2)
+            interleave(nc.scalar.copy, dy_bf, dy_raw[g], T // 2, T)
+            sort_plane((w8_plane, w4_plane)[g], (w8_plane_raw, w4_plane_raw)[g])
             quantize(dy_codes[g][:], dy_plane[g][:], dy_bf[:].rearrange("p c j -> p (c j)"), E5M2)
+            if g == 1:
+                for m in range(PACK):
+                    w4_pass(m)
 
             bu_bf = tile("bu_bf%d" % g, [P, PACK, P, PACK], BF16)
             interleave_by_slot(nc.vector.tensor_copy, bu_bf, bu_raw[g][:], 0, 2)
             interleave_by_slot(nc.scalar.copy, bu_bf, bu_raw[g][:], 2, PACK)
-            if g == 0:
-                sort_plane(w4_plane, w4_plane_raw)
             for s0 in (0, 2):
                 cols = slice(s0 * P, (s0 + 2) * P)
                 quantize(
@@ -137,44 +164,27 @@ def tile_mix_lrbwd_mix_mul_kernel(
                     start=(g == 0),
                     stop=(g == 1),
                 )
+            if g == 0:
+                nc.vector.tensor_copy(
+                    out=w4_codes[:].rearrange("p (u s m b) -> p u s m b", u=2, s=PACK, b=2),
+                    in_=w4_raw[:].rearrange("p (u m s b) -> p u s m b", u=2, s=PACK, b=2),
+                )
 
         nc.vector.tensor_copy(
             out=w8_codes[:].bitcast(I32).rearrange("p (u s m) -> p u m s", u=2, s=PACK),
             in_=w8_raw[:].bitcast(I32).rearrange("p (u m s) -> p u m s", u=2, s=PACK),
         )
-        nc.vector.tensor_copy(
-            out=w4_codes[:].rearrange("p (u s m b) -> p u s m b", u=2, s=PACK, b=2),
-            in_=w4_raw[:].rearrange("p (u m s b) -> p u s m b", u=2, s=PACK, b=2),
-        )
 
         h_sb = tile("h_sb", [P, PACK, T], F32)
         for s in range(PACK):
-            copy = nc.scalar.copy if s < PACK - 1 else nc.vector.tensor_copy
+            copy = nc.scalar.copy if s % 2 == 0 else nc.vector.tensor_copy
             copy(out=h_sb[:, s, :], in_=h_acc[s][:])
 
-        dx_acc = []
-        for m in range(TILES):
-            acc = ps.tile([P, T], F32, name="dx_acc%d" % m, tag="bank%d" % m)
-            dx_acc.append(acc)
-            cols = slice(m * P, (m + 1) * P)
-            nc.tensor.matmul_mx(
-                out=acc[:],
-                lhsT=w8_codes[:, cols].bitcast(E4M3),
-                lhsT_scale=w8_plane[:, cols],
-                rhs=dy_codes[0][:].bitcast(E5M2),
-                rhs_scale=dy_plane[0][:],
-                start=True,
-                stop=False,
-            )
-            nc.tensor.matmul_mx(
-                out=acc[:],
-                lhsT=w4_codes[:, 2 * m * P : 2 * (m + 1) * P].bitcast(E2M1),
-                lhsT_scale=w4_plane[:, cols],
-                rhs=dy_codes[1][:].bitcast(E5M2),
-                rhs_scale=dy_plane[1][:],
-                start=False,
-                stop=False,
-            )
+        for m in range(PACK):
+            w8_pass(m)
+        for m in range(PACK, TILES):
+            w4_pass(m)
+            w8_pass(m)
 
         h_bf = tile("h_bf", [P, T, PACK], BF16)
         h_codes = tile("h_codes", [P, T], U32)
@@ -211,9 +221,16 @@ def tile_mix_lrbwd_mix_mul_kernel(
                 start=False,
                 stop=True,
             )
-            nc.vector.tensor_tensor(
-                out=res[u][:, s, :], in0=acc[:], in1=d_sb[u][:, s, :], op=mybir.AluOpType.mult
-            )
+            if u == 1 and s % 2 == 0:
+                dx_sb = tile("dx_sb%d" % s, [P, T], F32)
+                nc.scalar.copy(out=dx_sb[:], in_=acc[:])
+                nc.gpsimd.tensor_tensor(
+                    out=res[u][:, s, :], in0=dx_sb[:], in1=d_sb[u][:, s, :], op=mybir.AluOpType.mult
+                )
+            else:
+                nc.vector.tensor_tensor(
+                    out=res[u][:, s, :], in0=acc[:], in1=d_sb[u][:, s, :], op=mybir.AluOpType.mult
+                )
 
         def store(u, s0, s1):
             rows = out_0[u * HALF : (u + 1) * HALF, :].rearrange("(p s) t -> p s t", s=PACK)
@@ -224,16 +241,16 @@ def tile_mix_lrbwd_mix_mul_kernel(
         quantize(h_codes[:], h_plane[:], h_bf[:].rearrange("p c j -> p (c j)"), E5M2)
         cast_ad(0)
         cast_ad(1)
-        quantize_ad(0, 0, PACK)
+        quantize_ad(0, 0, 2)
+        quantize_ad(0, 2, PACK)
         quantize_ad(1, 0, 2)
 
         nc.sync.dma_start(out=out_1.rearrange("(p s) t -> p s t", s=PACK), in_=h_sb[:])
 
-        for s in range(PACK):
-            finish(0, s)
-        store(0, 0, PACK)
-        quantize_ad(1, 2, PACK)
-        for s0 in (0, 2):
-            finish(1, s0)
-            finish(1, s0 + 1)
-            store(1, s0, s0 + 2)
+        for u in range(2):
+            for s0 in (0, 2):
+                finish(u, s0)
+                finish(u, s0 + 1)
+                store(u, s0, s0 + 2)
+                if (u, s0) == (0, 0):
+                    quantize_ad(1, 2, PACK)

@@ -46,7 +46,7 @@ def tile_mix_lrbwd_mix_mul_kernel(
         ctx.enter_context(tc.manual_schedule())
 
         def tile(name, shape, dtype):
-            return sb.tile(shape, dtype, name=name, tag=name, align_bytes=64)
+            return sb.tile(shape, dtype, name=name, tag=name, align_bytes=256)
 
         def quantize(codes, scales, grouped, fmt):
             nc.vector.quantize_mx(out=codes.bitcast(fmt), scales=scales, in_=grouped)

@@ -45,19 +45,22 @@ def tile_mix_lrbwd_mix_mul_kernel(
         ps = ctx.enter_context(tc.psum_pool(name="ps", bufs=1))
         ctx.enter_context(tc.manual_schedule())
 
-        def tile(name, shape, dtype):
-            return sb.tile(shape, dtype, name=name, tag=name, align_bytes=256)
+        def tile(name, shape, dtype, align=256):
+            return sb.tile(shape, dtype, name=name, tag=name, align_bytes=align)
+
+        def dma_tile(name, shape, dtype):
+            return tile(name, shape, dtype, align=4096)
 
         def quantize(codes, scales, grouped, fmt):
             nc.vector.quantize_mx(out=codes.bitcast(fmt), scales=scales, in_=grouped)
 
-        dy_raw = [tile("dy_raw%d" % g, [P, PACK, T], F32) for g in range(2)]
-        bu_raw = [tile("bu_raw%d" % g, [P, PACK, R], F32) for g in range(2)]
-        ad_raw = tile("ad_raw", [P, PACK, K], F32)
-        d_sb = [tile("d_sb%d" % u, [P, TILES // 2, T], F32) for u in range(2)]
-        w8_raw = tile("w8_raw", [P, K], U32)
-        w4_raw = tile("w4_raw", [P, 2 * K], U8)
-        planes_raw = tile("planes_raw", [P, 2 * K], U8)
+        dy_raw = [dma_tile("dy_raw%d" % g, [P, PACK, T], F32) for g in range(2)]
+        bu_raw = [dma_tile("bu_raw%d" % g, [P, PACK, R], F32) for g in range(2)]
+        ad_raw = dma_tile("ad_raw", [P, PACK, K], F32)
+        d_sb = [dma_tile("d_sb%d" % u, [P, TILES // 2, T], F32) for u in range(2)]
+        w8_raw = dma_tile("w8_raw", [P, K], U32)
+        w4_raw = dma_tile("w4_raw", [P, 2 * K], U8)
+        planes_raw = dma_tile("planes_raw", [P, 2 * K], U8)
         w8_plane_raw = planes_raw[:, 0:K]
         w4_plane_raw = planes_raw[:, K : 2 * K]
         w8_codes = tile("w8_codes", [P, K], U32)
@@ -175,7 +178,7 @@ def tile_mix_lrbwd_mix_mul_kernel(
             in_=w8_raw[:].bitcast(I32).rearrange("p (u m s) -> p u m s", u=2, s=PACK),
         )
 
-        h_sb = tile("h_sb", [P, PACK, T], F32)
+        h_sb = dma_tile("h_sb", [P, PACK, T], F32)
         for s in range(PACK):
             copy = nc.scalar.copy if s % 2 == 0 else nc.vector.tensor_copy
             copy(out=h_sb[:, s, :], in_=h_acc[s][:])
@@ -207,7 +210,7 @@ def tile_mix_lrbwd_mix_mul_kernel(
                 E4M3,
             )
 
-        res = [tile("res%d" % u, [P, PACK, T], F32) for u in range(2)]
+        res = [dma_tile("res%d" % u, [P, PACK, T], F32) for u in range(2)]
 
         def finish(u, s):
             acc = dx_acc[u * PACK + s]

@@ -253,7 +253,12 @@ def tile_mix_lrbwd_mix_mul_kernel(
         for u in range(2):
             for s0 in (0, 2):
                 finish(u, s0)
-                finish(u, s0 + 1)
-                store(u, s0, s0 + 2)
+                if (u, s0) == (0, 2):
+                    store(u, s0, s0 + 1)
+                    finish(u, s0 + 1)
+                    store(u, s0 + 1, s0 + 2)
+                else:
+                    finish(u, s0 + 1)
+                    store(u, s0, s0 + 2)
                 if (u, s0) == (0, 0):
                     quantize_ad(1, 2, PACK)

from contextlib import ExitStack

import concourse.mybir as mybir

N, R, K, T = 1024, 512, 1024, 512
FLOPS = 2 * (N * R * T + N * K * T + R * K * T)

F32 = mybir.dt.float32
BF16 = mybir.dt.bfloat16
I32 = mybir.dt.int32
U32 = mybir.dt.uint32
U8 = mybir.dt.uint8
E4M3 = mybir.dt.float8_e4m3fn_x4
E5M2 = mybir.dt.float8_e5m2_x4
E2M1 = mybir.dt.float4_e2m1fn_x4

P = 128
PACK = 4
PASS = P * PACK
HALF = K // 2
TILES = K // P
VECTOR_COLS = 352


def interleave(copy, grouped, raw, c0, c1):
    copy(
        out=grouped[:, c0:c1, :].rearrange("p (c i) j -> p c j i", i=4),
        in_=raw[:, :, c0:c1].rearrange("p j (c i) -> p c j i", i=4),
    )


def interleave_by_slot(copy, grouped, raw, s0, s1):
    copy(
        out=grouped[:, s0:s1, :, :].rearrange("p s m j -> p m j s"),
        in_=raw.rearrange("p j (m s) -> p m j s", s=PACK)[:, :, :, s0:s1],
    )


def tile_mix_lrbwd_mix_mul_kernel(
    tc, dy, w8_words, w8_scales, w4_words, w4_scales, bu, ad, d, out_0, out_1
):
    nc = tc.nc
    with ExitStack() as ctx:
        sb = ctx.enter_context(tc.tile_pool(name="sb", bufs=1))
        ps = ctx.enter_context(tc.psum_pool(name="ps", bufs=1))
        ctx.enter_context(tc.manual_schedule())

        def tile(name, shape, dtype, align=256):
            return sb.tile(shape, dtype, name=name, tag=name, align_bytes=align)

        def dma_tile(name, shape, dtype):
            return tile(name, shape, dtype, align=4096)

        def quantize(codes, scales, grouped, fmt):
            nc.vector.quantize_mx(out=codes.bitcast(fmt), scales=scales, in_=grouped)

        dy_raw = [dma_tile("dy_raw%d" % g, [P, PACK, T], F32) for g in range(2)]
        bu_raw = [dma_tile("bu_raw%d" % g, [P, PACK, R], F32) for g in range(2)]
        ad_raw = dma_tile("ad_raw", [P, PACK, K], F32)
        d_sb = [dma_tile("d_sb%d" % u, [P, TILES // 2, T], F32) for u in range(2)]
        w8_raw = dma_tile("w8_raw", [P, K], U32)
        w4_raw = dma_tile("w4_raw", [P, 2 * K], U8)
        planes_raw = dma_tile("planes_raw", [P, 2 * K], U8)
        w8_plane_raw = planes_raw[:, 0:K]
        w4_plane_raw = planes_raw[:, K : 2 * K]
        w8_codes = tile("w8_codes", [P, K], U32)
        w4_codes = tile("w4_codes", [P, 2 * K], U8)
        w8_plane = tile("w8_plane", [P, K], U8)
        w4_plane = tile("w4_plane", [P, K], U8)

        nc.vector.memset(planes_raw[:].bitcast(U32), 0)

        def load_rows(dst, rows):
            nc.sync.dma_start(out=dst[:], in_=rows.rearrange("(p j) c -> p j c", j=PACK))

        def load_scale_rows(plane, scales, q):
            nc.sync.dma_start(
                out=plane[q:P:32, :].bitcast(I32),
                in_=scales[0, q:16:4, :].bitcast(I32),
            )

        load_rows(dy_raw[0], dy[0:PASS, :])
        for q in range(4):
            load_scale_rows(w8_plane_raw, w8_scales, q)
        load_rows(bu_raw[0], bu[0:PASS, :])
        nc.sync.dma_start(out=w4_raw[:].bitcast(I32), in_=w4_words[0].bitcast(I32))
        load_rows(dy_raw[1], dy[PASS:N, :])
        for q in range(4):
            load_scale_rows(w4_plane_raw, w4_scales, q)
        load_rows(bu_raw[1], bu[PASS:N, :])
        nc.sync.dma_start(
            out=w8_raw[:].bitcast(I32),
            in_=w8_words[0].rearrange("p k i -> p (k i)").bitcast(I32),
        )
        load_rows(ad_raw, ad)
        for u in range(2):
            load_rows(d_sb[u], d[u * HALF : (u + 1) * HALF, :])

        def sort_plane(plane, raw):
            nc.vector.tensor_copy(
                out=plane[:].rearrange("p (u s m) -> p u s m", u=2, s=PACK),
                in_=raw.rearrange("p (u m s) -> p u s m", u=2, s=PACK),
            )

        dy_codes = [tile("dy_codes%d" % g, [P, T], U32) for g in range(2)]
        dy_plane = [tile("dy_plane%d" % g, [P, T], U8) for g in range(2)]
        bu_codes = [tile("bu_codes%d" % g, [P, R], U32) for g in range(2)]
        bu_plane = [tile("bu_plane%d" % g, [P, R], U8) for g in range(2)]
        h_acc = [ps.tile([P, T], F32, name="h_acc%d" % s, tag="bank%d" % (4 + s)) for s in range(PACK)]

        dx_acc = []

        def w4_pass(m):
            acc = ps.tile([P, T], F32, name="dx_acc%d" % m, tag="bank%d" % m)
            dx_acc.append(acc)
            nc.tensor.matmul_mx(
                out=acc[:],
                lhsT=w4_codes[:, 2 * m * P : 2 * (m + 1) * P].bitcast(E2M1),
                lhsT_scale=w4_plane[:, m * P : (m + 1) * P],
                rhs=dy_codes[1][:].bitcast(E5M2),
                rhs_scale=dy_plane[1][:],
                start=True,
                stop=False,
            )

        def w8_pass(m):
            cols = slice(m * P, (m + 1) * P)
            nc.tensor.matmul_mx(
                out=dx_acc[m][:],
                lhsT=w8_codes[:, cols].bitcast(E4M3),
                lhsT_scale=w8_plane[:, cols],
                rhs=dy_codes[0][:].bitcast(E5M2),
                rhs_scale=dy_plane[0][:],
                start=False,
                stop=False,
            )

        for g in range(2):
            dy_bf = tile("dy_bf%d" % g, [P, T, PACK], BF16)
            interleave(nc.vector.tensor_copy, dy_bf, dy_raw[g], 0, T // 2)
            interleave(nc.scalar.copy, dy_bf, dy_raw[g], T // 2, T)
            sort_plane((w8_plane, w4_plane)[g], (w8_plane_raw, w4_plane_raw)[g])
            quantize(dy_codes[g][:], dy_plane[g][:], dy_bf[:].rearrange("p c j -> p (c j)"), E5M2)
            if g == 1:
                for m in range(PACK):
                    w4_pass(m)

            bu_bf = tile("bu_bf%d" % g, [P, PACK, P, PACK], BF16)
            interleave_by_slot(nc.vector.tensor_copy, bu_bf, bu_raw[g][:], 0, 2)
            interleave_by_slot(nc.scalar.copy, bu_bf, bu_raw[g][:], 2, PACK)
            for s0 in (0, 2):
                cols = slice(s0 * P, (s0 + 2) * P)
                quantize(
                    bu_codes[g][:, cols],
                    bu_plane[g][:, cols],
                    bu_bf[:, s0 : s0 + 2, :, :].rearrange("p s m j -> p (s m j)"),
                    E4M3,
                )
            for s in range(PACK):
                cols = slice(s * P, (s + 1) * P)
                nc.tensor.matmul_mx(
                    out=h_acc[s][:],
                    lhsT=bu_codes[g][:, cols].bitcast(E4M3),
                    lhsT_scale=bu_plane[g][:, cols],
                    rhs=dy_codes[g][:].bitcast(E5M2),
                    rhs_scale=dy_plane[g][:],
                    start=(g == 0),
                    stop=(g == 1),
                )
            if g == 0:
                nc.vector.tensor_copy(
                    out=w4_codes[:].rearrange("p (u s m b) -> p u s m b", u=2, s=PACK, b=2),
                    in_=w4_raw[:].rearrange("p (u m s b) -> p u s m b", u=2, s=PACK, b=2),
                )

        nc.vector.tensor_copy(
            out=w8_codes[:].bitcast(I32).rearrange("p (u s m) -> p u m s", u=2, s=PACK),
            in_=w8_raw[:].bitcast(I32).rearrange("p (u m s) -> p u m s", u=2, s=PACK),
        )

        h_sb = dma_tile("h_sb", [P, PACK, T], F32)
        for s in range(PACK):
            copy = nc.scalar.copy if s % 2 == 0 else nc.vector.tensor_copy
            copy(out=h_sb[:, s, :], in_=h_acc[s][:])

        for m in range(PACK):
            w8_pass(m)
        for m in range(PACK, TILES):
            w4_pass(m)
            w8_pass(m)

        h_bf = tile("h_bf", [P, T, PACK], BF16)
        h_codes = tile("h_codes", [P, T], U32)
        h_plane = tile("h_plane", [P, T], U8)
        ad_bf = [tile("ad_bf%d" % u, [P, PACK, P, PACK], BF16) for u in range(2)]
        ad_codes = [tile("ad_codes%d" % u, [P, HALF], U32) for u in range(2)]
        ad_plane = [tile("ad_plane%d" % u, [P, HALF], U8) for u in range(2)]

        def cast_ad(u):
            raw = ad_raw[:, :, u * HALF : (u + 1) * HALF]
            interleave_by_slot(nc.vector.tensor_copy, ad_bf[u], raw, 0, 2)
            interleave_by_slot(nc.scalar.copy, ad_bf[u], raw, 2, PACK)

        def quantize_ad(u, s0, s1):
            cols = slice(s0 * P, s1 * P)
            quantize(
                ad_codes[u][:, cols],
                ad_plane[u][:, cols],
                ad_bf[u][:, s0:s1, :, :].rearrange("p s m j -> p (s m j)"),
                E4M3,
            )

        res = [dma_tile("res%d" % u, [P, PACK, T], F32) for u in range(2)]

        def finish(u, s):
            acc = dx_acc[u * PACK + s]
            cols = slice(s * P, (s + 1) * P)
            nc.tensor.matmul_mx(
                out=acc[:],
                lhsT=ad_codes[u][:, cols].bitcast(E4M3),
                lhsT_scale=ad_plane[u][:, cols],
                rhs=h_codes[:].bitcast(E5M2),
                rhs_scale=h_plane[:],
                start=False,
                stop=True,
            )
            if u == 1 and s % 2 == 0:
                dx_sb = tile("dx_sb%d" % s, [P, T], F32)
                nc.scalar.copy(out=dx_sb[:], in_=acc[:])
                nc.gpsimd.tensor_tensor(
                    out=res[u][:, s, :], in0=dx_sb[:], in1=d_sb[u][:, s, :], op=mybir.AluOpType.mult
                )
            else:
                nc.vector.tensor_tensor(
                    out=res[u][:, s, :], in0=acc[:], in1=d_sb[u][:, s, :], op=mybir.AluOpType.mult
                )

        def store(u, s0, s1):
            rows = out_0[u * HALF : (u + 1) * HALF, :].rearrange("(p s) t -> p s t", s=PACK)
            nc.sync.dma_start(out=rows[:, s0:s1, :], in_=res[u][:, s0:s1, :])

        interleave(nc.vector.tensor_copy, h_bf, h_sb, 0, VECTOR_COLS)
        interleave(nc.scalar.copy, h_bf, h_sb, VECTOR_COLS, T)
        quantize(h_codes[:], h_plane[:], h_bf[:].rearrange("p c j -> p (c j)"), E5M2)
        cast_ad(0)
        cast_ad(1)
        quantize_ad(0, 0, 2)
        quantize_ad(0, 2, PACK)
        quantize_ad(1, 0, 2)

        nc.sync.dma_start(out=out_1.rearrange("(p s) t -> p s t", s=PACK), in_=h_sb[:])

        for u in range(2):
            for s0 in (0, 2):
                finish(u, s0)
                if (u, s0) == (0, 2):
                    store(u, s0, s0 + 1)
                    finish(u, s0 + 1)
                    store(u, s0 + 1, s0 + 2)
                else:
                    finish(u, s0 + 1)
                    store(u, s0, s0 + 2)
                if (u, s0) == (0, 0):
                    quantize_ad(1, 2, PACK)
